import numpy as np
import ml_dtypes


def mxq(x, axis, fmt="e4m3"):
    dtype, down = {"e4m3": (ml_dtypes.float8_e4m3fn, 7), "e5m2": (ml_dtypes.float8_e5m2, 14)}[fmt]
    v = np.moveaxis(np.asarray(x, np.float32).astype(ml_dtypes.bfloat16).astype(np.float64), axis, -1)
    blocks = v.reshape(v.shape[:-1] + (-1, 32))
    amax = np.abs(blocks).max(-1, keepdims=True)
    byte = np.maximum(np.where(amax > 0, np.frexp(amax)[1] - 1 + 127, 0) - down, 1)
    scale = np.exp2(byte - 127.0)
    codes = (blocks / scale).astype(np.float32).astype(dtype).astype(np.float64)
    return np.moveaxis((codes * scale).reshape(v.shape), -1, axis)


WIDE = False


def mx_kscale(k):
    if not WIDE:
        return np.ones(k)
    levels = np.array([10, -10, 5, -5, 0])
    if k % 512:
        return np.exp2(np.random.permutation(np.resize(levels, k // 32))).repeat(32)
    a = np.empty((k // 512, 16))
    for p in range(k // 512):
        a[p, :8] = np.random.permutation(np.resize(levels, 8))
        for g in range(8):
            far = levels[np.abs(levels - a[p, g]) >= 10]
            a[p, g + 8] = far[np.random.randint(len(far))]
    return np.exp2(a.ravel()).repeat(32)


def f64(x):
    return np.asarray(x).astype(np.float64)


def striped(idx):
    return np.tile(idx.reshape(-1, 16).T, (8, 1)).astype(np.uint16)


def unstriped(offs):
    return offs[:16].T.reshape(-1).astype(np.int64)


def striped8(idx):
    return np.concatenate([x.reshape(-1, 16).T for x in idx]).astype(np.uint16)


def runs(offs, k):
    lists = np.stack([offs[16 * r : 16 * r + 16].T.reshape(-1) for r in range(8)]).astype(np.int64)
    return lists[np.arange(k) % 512 // 64]


def pack_weight(w):
    k, n = w.shape
    w = f64(np.asarray(w, np.float32).astype(ml_dtypes.bfloat16)).reshape(k // 32, 32, n)
    amax = np.abs(w).max(1)
    byte = np.clip(np.where(amax > 0, np.frexp(amax)[1] - 1 + 127 - 7, 1), 1, 254)
    scaled = (w * np.exp2(127.0 - byte)[:, None, :]).reshape(k, n).astype(np.float32)
    words = np.ascontiguousarray(scaled.reshape(k // 512, 128, 4, n).transpose(0, 1, 3, 2)).astype(ml_dtypes.float8_e4m3fn).view(np.uint8)
    return words, np.ascontiguousarray(byte.astype(np.uint8).reshape(k // 512, 16, n))


def unpack_weight(words, scales):
    g, p, n, _ = words.shape
    vals = np.ascontiguousarray(words).view(ml_dtypes.float8_e4m3fn).astype(np.float64) * np.repeat(np.exp2(scales.astype(np.float64) - 127.0), 8, axis=1)[..., None]
    return vals.transpose(0, 1, 3, 2).reshape(g * 512, n)


K, T, S, N, H = 512, 2048, 512, 512, 512


def setup_inputs():
    n = np.random.standard_normal
    s = mx_kscale(K)[:, None]
    u = mx_kscale(H)
    packed_xT = pack_weight(n((K, T)) * s)
    return {
        "x_words": packed_xT[0],
        "x_scales": packed_xT[1],
        "w1": (n((K, H)) / np.sqrt(K) / s).astype(np.float32),
        "gn": (np.random.uniform(0.5, 1.5, (H, 1)) * u[:, None]).astype(np.float32),
        "w2": (n((H, H)) / np.sqrt(H) / u[:, None]).astype(np.float32),
        "res": n((N, S)).astype(np.float32),
        "w3": (n((H, N)) / np.sqrt(H) / u[:, None]).astype(np.float32),
        "offs": striped(np.random.permutation(T)[:S]),
        "nx": striped8(np.random.randint(0, S, (8, S))),
        "mv": striped8(np.stack([np.random.permutation(S) for _ in range(8)])),
    }


def reference(x_words, x_scales, w1, gn, w2, res, w3, offs, nx, mv):
    xq = unpack_weight(x_words, x_scales)[:, unstriped(offs)]
    y = mxq(f64(w1), 0, "e4m3").T @ xq
    p = y + y[np.arange(H)[:, None], runs(nx, H)]
    r2 = np.maximum(p, p[np.arange(H)[:, None], runs(nx, H)])
    z = f64(gn) * (r2 - (r2[np.arange(H)[:, None], runs(nx, H)]))
    h = np.tanh(mxq(f64(w2), 0, "e4m3").T @ mxq(z, 0, "e4m3"))
    z2 = f64(gn) * (h[np.arange(H)[:, None], runs(mv, H)])
    return f64(res) + (mxq(f64(w3), 0, "e4m3").T @ mxq(z2, 0, "e4m3"))

@@ -1,0 +1,218 @@
+from contextlib import ExitStack
+
+import concourse.mybir as mybir
+
+K, T, S, H, N = 512, 2048, 512, 512, 512
+FLOPS = 2 * K * H * S + 2 * H * H * S + 2 * H * N * S
+
+F32 = mybir.dt.float32
+BF16 = mybir.dt.bfloat16
+I32 = mybir.dt.int32
+U32 = mybir.dt.uint32
+U16 = mybir.dt.uint16
+U8 = mybir.dt.uint8
+FP8X4 = mybir.dt.float8_e4m3fn_x4
+ALU = mybir.AluOpType
+ACT = mybir.ActivationFunctionType
+
+P = 128
+PACK = 4
+HALF = S // 2
+PIECES = ((0, 128), (128, 256), (384, 128))
+OUT_PIECES = ((0, 256), (256, 128), (384, 128))
+W1_SCALAR_SHARE = 40
+
+
+def tile_picked_alldbl3_none_p_kernel(
+    tc, x_words, x_scales, w1, gn, w2, res, w3, offs, nx, mv, out
+):
+    nc = tc.nc
+    with ExitStack() as ctx:
+        sb = ctx.enter_context(tc.tile_pool(name="sb", bufs=1))
+        ps = ctx.enter_context(tc.psum_pool(name="ps", bufs=1))
+
+        def tile(name, shape, dtype):
+            return sb.tile(shape, dtype, name=name, align_bytes=64)
+
+        def bank(number, name):
+            return ps.tile([P, 512], F32, name=name, tag=f"bank{number}")
+
+        def entries(lists, start, count):
+            return lists[:, start // 16 : (start + count) // 16]
+
+        def fetch(engine, dst, window, lists, start, count):
+            src = window[:].indirect(entries(lists, start, count))
+            if engine is nc.vector:
+                nc.vector.tensor_copy(out=dst, in_=src)
+            else:
+                nc.scalar.activation(out=dst, in_=src, func=ACT.Copy)
+
+        def quantize(name, values, width):
+            codes = tile(name + "_codes", [P, width], U32)
+            scales = tile(name + "_scales", [P, width], U8)
+            nc.vector.quantize_mx(out=codes[:].bitcast(FP8X4), scales=scales[:], in_=values)
+            return codes, scales
+
+        def product(dst, weights, t, codes, scales):
+            cols = slice(P * t, P * (t + 1))
+            nc.tensor.matmul_mx(
+                out=dst,
+                lhsT=weights[0][:, cols].bitcast(FP8X4),
+                lhsT_scale=weights[1][:, cols],
+                rhs=codes.bitcast(FP8X4),
+                rhs_scale=scales,
+                start=True,
+                stop=True,
+            )
+
+        offs_sb = sb.tile([P, S // 16], U16, name="offs_sb")
+        nx_sb = sb.tile([P, S // 16], U16, name="nx_sb")
+        mv_sb = sb.tile([P, S // 16], U16, name="mv_sb")
+        x_sb = tile("x_sb", [P, T], I32)
+        xs_sb = tile("xs_sb", [P, T], U8)
+        gain = tile("gain", [P, PACK], F32)
+        raw = [tile(f"raw{i}", [P, PACK, 512], F32) for i in range(3)]
+        res_sb = [tile(f"res{i}", [P, PACK, width], F32) for i, (start, width) in enumerate(OUT_PIECES)]
+
+        nc.vector.memset(xs_sb[:].bitcast(I32), 0)
+        nc.sync.dma_start(offs_sb[:], offs)
+        nc.sync.dma_start(raw[0][:], w1.rearrange("(p j) c -> p j c", j=PACK))
+        for q in range(4):
+            nc.sync.dma_start(
+                xs_sb[32 * q : 32 * q + 4, :].bitcast(I32), x_scales[0, 4 * q : 4 * q + 4, :].bitcast(I32)
+            )
+        nc.sync.dma_start(x_sb[:], x_words[0].rearrange("p c r -> p (c r)").bitcast(I32))
+        nc.sync.dma_start(nx_sb[:], nx)
+        nc.sync.dma_start(raw[1][:], w2.rearrange("(p j) c -> p j c", j=PACK))
+        nc.sync.dma_start(gain[:], gn.rearrange("(p t) o -> p (t o)", t=PACK))
+        nc.sync.dma_start(raw[2][:], w3.rearrange("(p j) c -> p j c", j=PACK))
+        nc.sync.dma_start(mv_sb[:], mv)
+        res_rows = res.rearrange("(t p) c -> p t c", p=P)
+        out_rows = out.rearrange("(t p) c -> p t c", p=P)
+        for i, (start, width) in enumerate(OUT_PIECES):
+            nc.sync.dma_start(res_sb[i][:], res_rows[:, :, start : start + width])
+
+        def dealt_views(i, rounded):
+            dst = rounded[:].rearrange("p (t m j) -> p m j t", t=PACK, j=PACK)
+            src = raw[i][:].rearrange("p j (m t) -> p m j t", t=PACK)
+            return dst, src
+
+        xq_scales = tile("xq_scales", [P, S], U8)
+        nc.vector.tensor_copy(out=xq_scales[:], in_=xs_sb[:].indirect(offs_sb[:]))
+
+        w1_bf = tile("w1_bf", [P, PACK * H], BF16)
+        dst, src = dealt_views(0, w1_bf)
+        nc.scalar.copy(out=dst[:, :W1_SCALAR_SHARE], in_=src[:, :W1_SCALAR_SHARE])
+        nc.vector.tensor_copy(out=dst[:, W1_SCALAR_SHARE:], in_=src[:, W1_SCALAR_SHARE:])
+        w1q = quantize("w1", w1_bf[:], H)
+
+        xq = [tile(f"xq{h}", [P, HALF], U32) for h in range(2)]
+        for h in range(2):
+            nc.vector.tensor_copy(out=xq[h][:], in_=x_sb[:].bitcast(U32).indirect(entries(offs_sb, h * HALF, HALF)))
+
+        halves = [slice(h * HALF, (h + 1) * HALF) for h in range(2)]
+        y = [tile(f"y{t}", [P, S], F32) for t in range(PACK)]
+        y_ps = {}
+        for h, t in ((0, 0), (0, 1), (1, 0), (1, 1), (0, 2), (1, 2), (0, 3), (1, 3)):
+            y_ps[h, t] = bank(2 * t + h, f"y_ps{h}{t}")[:, :HALF]
+            product(y_ps[h, t], w1q, t, xq[h][:], xq_scales[:, halves[h]])
+            if h == 0 and t < 2:
+                nc.scalar.copy(out=y[t][:, halves[h]], in_=y_ps[h, t])
+            else:
+                nc.vector.tensor_copy(out=y[t][:, halves[h]], in_=y_ps[h, t])
+
+        y_next = [tile(f"y_next{t}", [P, S], F32) for t in range(PACK)]
+        for t in range(PACK):
+            for h in range(2):
+                fetch(nc.vector if t == 3 else nc.scalar, y_next[t][:, halves[h]], y[t], nx_sb, h * HALF, HALF)
+
+        p = [tile(f"p{t}", [P, S], F32) for t in range(PACK)]
+        p_next = [tile(f"p_next{t}", [P, S], F32) for t in range(PACK)]
+        for t in (0, 1, 3, 2):
+            for h in range(2):
+                nc.vector.tensor_tensor(out=p[t][:, halves[h]], in0=y_ps[h, t], in1=y_next[t][:, halves[h]], op=ALU.add)
+        for t in (0, 1, 3, 2):
+            for h in range(2):
+                fetch(nc.scalar, p_next[t][:, halves[h]], p[t], nx_sb, h * HALF, HALF)
+
+        w2_bf = tile("w2_bf", [P, PACK * H], BF16)
+        dst, src = dealt_views(1, w2_bf)
+        r2 = [tile(f"r2{t}", [P, S], F32) for t in range(PACK)]
+        for step, t in enumerate((0, 1, 3, 2)):
+            if step < 2:
+                part = slice(64 * step, 64 * (step + 1))
+                nc.vector.tensor_copy(out=dst[:, part], in_=src[:, part])
+            if step == 2:
+                w2q = quantize("w2", w2_bf[:], H)
+            nc.vector.tensor_tensor(out=r2[t][:], in0=p[t][:], in1=p_next[t][:], op=ALU.max)
+
+        def gained(name, planes, width):
+            rounded = tile(name + "_bf", [P, PACK * width], BF16)
+            nc.vector.tensor_tensor(
+                out=rounded[:].rearrange("p (c i t) -> p c t i", t=PACK, i=4),
+                in0=planes[:].rearrange("p t (c i) -> p c t i", i=4),
+                in1=gain[:].unsqueeze(1).unsqueeze(3).to_broadcast([P, width // 4, PACK, 4]),
+                op=ALU.mult,
+            )
+            return rounded
+
+        def piece_banks(first, name, i, width):
+            per_bank = 512 // width
+            banks = [bank(first + b, f"{name}{i}{b}") for b in range(PACK // per_bank)]
+            return banks, per_bank
+
+        hid = [tile(f"h{t}", [P, S], F32) for t in range(PACK)]
+        first_bank = (0, 1, 3)
+        later = []
+        for i, (start, width) in enumerate(PIECES):
+            cols = slice(start, start + width)
+            diff = tile(f"diff{i}", [P, PACK, width], F32)
+            for t in (0, 1, 3, 2):
+                r2_next = tile(f"r2_next{t}", [P, width], F32)
+                fetch(nc.scalar, r2_next[:], r2[t], nx_sb, start, width)
+                nc.vector.tensor_tensor(out=diff[:, t, :], in0=r2[t][:, cols], in1=r2_next[:], op=ALU.subtract)
+            z_bf = gained(f"z{i}", diff, width)
+            codes, scales = quantize(f"z{i}", z_bf[:], width)
+            banks, per_bank = piece_banks(first_bank[i], "h_ps", i, width)
+            for t in range(PACK):
+                acc = banks[t // per_bank][:, (t % per_bank) * width : (t % per_bank + 1) * width]
+                product(acc, w2q, t, codes[:], scales[:])
+                later.append((hid[t][:, cols], acc))
+        for dst_h, acc in later:
+            nc.scalar.activation(out=dst_h, in_=acc, func=ACT.Tanh)
+
+        w3_bf = tile("w3_bf", [P, PACK * N], BF16)
+        nc.vector.tensor_copy(
+            out=w3_bf[:].rearrange("p (c i j) -> p c j i", j=PACK, i=4),
+            in_=raw[2][:].rearrange("p j (c i) -> p c j i", i=4),
+        )
+        w3q = quantize("w3", w3_bf[:], N)
+
+        def finish(i, banks, per_bank):
+            start, width = OUT_PIECES[i]
+            result = tile(f"result{i}", [P, PACK, width], F32)
+            for b, acc in enumerate(banks):
+                rows = slice(b * per_bank, (b + 1) * per_bank)
+                nc.vector.tensor_tensor(
+                    out=result[:, rows, :].rearrange("p t c -> p (t c)"),
+                    in0=acc[:],
+                    in1=res_sb[i][:, rows, :].rearrange("p t c -> p (t c)"),
+                    op=ALU.add,
+                )
+                nc.sync.dma_start(out_rows[:, rows, start : start + width], result[:, rows, :])
+
+        pending = None
+        for i, (start, width) in enumerate(OUT_PIECES):
+            moved = tile(f"moved{i}", [P, PACK, width], F32)
+            for t in range(PACK):
+                fetch(nc.vector if i == 0 and t < 2 else nc.scalar, moved[:, t, :], hid[t], mv_sb, start, width)
+            z2_bf = gained(f"z2{i}", moved, width)
+            codes, scales = quantize(f"z2{i}", z2_bf[:], width)
+            banks, per_bank = piece_banks((4, 6, 7)[i], "o_ps", i, width)
+            for t in range(PACK):
+                acc = banks[t // per_bank][:, (t % per_bank) * width : (t % per_bank + 1) * width]
+                product(acc, w3q, t, codes[:], scales[:])
+            if pending is not None:
+                finish(*pending)
+            pending = (i, banks, per_bank)
+        finish(*pending)

@@ -18,9 +18,9 @@ ACT = mybir.ActivationFunctionType
 P = 128
 PACK = 4
 HALF = S // 2
-PIECES = ((0, 128), (128, 256), (384, 128))
+PIECES = ((0, 256), (256, 128), (384, 128))
 OUT_PIECES = ((0, 256), (256, 128), (384, 128))
-W1_SCALAR_SHARE = 40
+W1_SCALAR_SHARE = 64
 
 
 def tile_picked_alldbl3_none_p_kernel(
@@ -106,113 +106,204 @@ def tile_picked_alldbl3_none_p_kernel(
         nc.vector.tensor_copy(out=dst[:, W1_SCALAR_SHARE:], in_=src[:, W1_SCALAR_SHARE:])
         w1q = quantize("w1", w1_bf[:], H)
 
-        xq = [tile(f"xq{h}", [P, HALF], U32) for h in range(2)]
-        for h in range(2):
-            nc.vector.tensor_copy(out=xq[h][:], in_=x_sb[:].bitcast(U32).indirect(entries(offs_sb, h * HALF, HALF)))
-
+        xq = tile("xq", [P, S], U32)
         halves = [slice(h * HALF, (h + 1) * HALF) for h in range(2)]
+        for h in range(2):
+            nc.vector.tensor_copy(out=xq[:, halves[h]], in_=x_sb[:].bitcast(U32).indirect(entries(offs_sb, h * HALF, HALF)))
+
         y = [tile(f"y{t}", [P, S], F32) for t in range(PACK)]
-        y_ps = {}
-        for h, t in ((0, 0), (0, 1), (1, 0), (1, 1), (0, 2), (1, 2), (0, 3), (1, 3)):
-            y_ps[h, t] = bank(2 * t + h, f"y_ps{h}{t}")[:, :HALF]
-            product(y_ps[h, t], w1q, t, xq[h][:], xq_scales[:, halves[h]])
-            if h == 0 and t < 2:
-                nc.scalar.copy(out=y[t][:, halves[h]], in_=y_ps[h, t])
+        y_parts = [(0, halves[0]), (1, halves[0]), (0, halves[1]), (1, halves[1]), (2, slice(0, S)), (3, slice(0, S))]
+        y_ps = []
+        for b, (t, cols) in enumerate(y_parts):
+            y_ps.append(bank(b, f"y_ps{b}")[:, cols])
+            product(y_ps[b], w1q, t, xq[:, cols], xq_scales[:, cols])
+            if b in (0, 1):
+                nc.scalar.copy(out=y[t][:, cols], in_=y_ps[b])
             else:
-                nc.vector.tensor_copy(out=y[t][:, halves[h]], in_=y_ps[h, t])
+                nc.vector.tensor_copy(out=y[t][:, cols], in_=y_ps[b])
 
         y_next = [tile(f"y_next{t}", [P, S], F32) for t in range(PACK)]
-        for t in range(PACK):
-            for h in range(2):
-                fetch(nc.vector if t == 3 else nc.scalar, y_next[t][:, halves[h]], y[t], nx_sb, h * HALF, HALF)
 
         p = [tile(f"p{t}", [P, S], F32) for t in range(PACK)]
         p_next = [tile(f"p_next{t}", [P, S], F32) for t in range(PACK)]
-        for t in (0, 1, 3, 2):
-            for h in range(2):
-                nc.vector.tensor_tensor(out=p[t][:, halves[h]], in0=y_ps[h, t], in1=y_next[t][:, halves[h]], op=ALU.add)
-        for t in (0, 1, 3, 2):
-            for h in range(2):
-                fetch(nc.scalar, p_next[t][:, halves[h]], p[t], nx_sb, h * HALF, HALF)
+        def gained(dst, src, t):
+            nc.vector.tensor_scalar(out=dst, in0=src, scalar1=gain[:, t : t + 1], scalar2=None, op0=ALU.mult)
 
-        w2_bf = tile("w2_bf", [P, PACK * H], BF16)
-        dst, src = dealt_views(1, w2_bf)
-        r2 = [tile(f"r2{t}", [P, S], F32) for t in range(PACK)]
-        for step, t in enumerate((0, 1, 3, 2)):
-            if step < 2:
-                part = slice(64 * step, 64 * (step + 1))
-                nc.vector.tensor_copy(out=dst[:, part], in_=src[:, part])
-            if step == 2:
-                w2q = quantize("w2", w2_bf[:], H)
-            nc.vector.tensor_tensor(out=r2[t][:], in0=p[t][:], in1=p_next[t][:], op=ALU.max)
-
-        def gained(name, planes, width):
-            rounded = tile(name + "_bf", [P, PACK * width], BF16)
-            nc.vector.tensor_tensor(
+        def woven(name, planes, width):
+            rounded = tile(name, [P, PACK * width], BF16)
+            nc.vector.tensor_copy(
                 out=rounded[:].rearrange("p (c i t) -> p c t i", t=PACK, i=4),
-                in0=planes[:].rearrange("p t (c i) -> p c t i", i=4),
-                in1=gain[:].unsqueeze(1).unsqueeze(3).to_broadcast([P, width // 4, PACK, 4]),
-                op=ALU.mult,
+                in_=planes[:].rearrange("p t (c i) -> p c t i", i=4),
             )
             return rounded
 
-        def piece_banks(first, name, i, width):
-            per_bank = 512 // width
-            banks = [bank(first + b, f"{name}{i}{b}") for b in range(PACK // per_bank)]
-            return banks, per_bank
+        w2_bf = tile("w2_bf", [P, PACK * H], BF16)
+        w3_bf = tile("w3_bf", [P, PACK * N], BF16)
+        r2 = [tile(f"r2{t}", [P, S], F32) for t in range(PACK)]
+        larger = [tile(f"larger{t}", [P, S], F32) for t in range(PACK)]
+
+        def round_w2(part):
+            dst, src = dealt_views(1, w2_bf)
+            cols = slice(64 * part, 64 * (part + 1))
+            nc.vector.tensor_copy(out=dst[:, cols], in_=src[:, cols])
+
+        def round_w3(part):
+            dst = w3_bf[:].rearrange("p (c i j) -> p c j i", j=PACK, i=4)
+            src = raw[2][:].rearrange("p j (c i) -> p c j i", i=4)
+            cols = slice(32 * part, 32 * (part + 1))
+            nc.vector.tensor_copy(out=dst[:, cols], in_=src[:, cols])
+
+        def fetch_y(engine, t):
+            for h in range(2):
+                fetch(engine, y_next[t][:, halves[h]], y[t], nx_sb, h * HALF, HALF)
+
+        def add_next(t, only=None):
+            for b, (part_t, cols) in enumerate(y_parts):
+                if part_t == t and only in (None, b):
+                    nc.vector.tensor_tensor(out=p[t][:, cols], in0=y_ps[b], in1=y_next[t][:, cols], op=ALU.add)
+
+        def fetch_p(engine, t):
+            for h in range(2):
+                fetch(engine, p_next[t][:, halves[h]], p[t], nx_sb, h * HALF, HALF)
+
+        def keep_larger(t):
+            nc.vector.tensor_tensor(out=larger[t][:], in0=p[t][:], in1=p_next[t][:], op=ALU.max)
+
+        def gain_r2(t):
+            gained(r2[t][:], larger[t][:], t)
 
         hid = [tile(f"h{t}", [P, S], F32) for t in range(PACK)]
-        first_bank = (0, 1, 3)
-        later = []
-        for i, (start, width) in enumerate(PIECES):
-            cols = slice(start, start + width)
-            diff = tile(f"diff{i}", [P, PACK, width], F32)
-            for t in (0, 1, 3, 2):
-                r2_next = tile(f"r2_next{t}", [P, width], F32)
-                fetch(nc.scalar, r2_next[:], r2[t], nx_sb, start, width)
-                nc.vector.tensor_tensor(out=diff[:, t, :], in0=r2[t][:, cols], in1=r2_next[:], op=ALU.subtract)
-            z_bf = gained(f"z{i}", diff, width)
-            codes, scales = quantize(f"z{i}", z_bf[:], width)
-            banks, per_bank = piece_banks(first_bank[i], "h_ps", i, width)
+        plain = [tile(f"tanh{t}", [P, S], F32) for t in range(PACK)]
+        diff = [tile(f"diff{i}", [P, PACK, width], BF16) for i, (start, width) in enumerate(PIECES)]
+        moved = [tile(f"moved{i}", [P, PACK, width], BF16) for i, (start, width) in enumerate(OUT_PIECES)]
+        rounded = {}
+        sums = {}
+        wq = {}
+
+        def subtract_next(engine, i, t):
+            start, width = PIECES[i]
+            r2_next = tile(f"r2_next{t}", [P, width], F32)
+            fetch(engine, r2_next[:], r2[t], nx_sb, start, width)
+            nc.vector.tensor_tensor(out=diff[i][:, t, :], in0=r2[t][:, start : start + width], in1=r2_next[:], op=ALU.subtract)
+
+        def weave(name, planes, width):
+            rounded[name] = woven(name + "_bf", planes, width)
+
+        def multiply(name, weights, width, first):
+            codes, scales = quantize(name, rounded[name][:], width)
+            per_bank = 512 // width
+            banks = [bank(first + b, f"{name}_ps{b}") for b in range(PACK // per_bank)]
+            sums[name] = banks
+            accs = []
             for t in range(PACK):
-                acc = banks[t // per_bank][:, (t % per_bank) * width : (t % per_bank + 1) * width]
-                product(acc, w2q, t, codes[:], scales[:])
-                later.append((hid[t][:, cols], acc))
-        for dst_h, acc in later:
-            nc.scalar.activation(out=dst_h, in_=acc, func=ACT.Tanh)
+                accs.append(banks[t // per_bank][:, (t % per_bank) * width : (t % per_bank + 1) * width])
+                product(accs[t], weights, t, codes[:], scales[:])
+            return accs
 
-        w3_bf = tile("w3_bf", [P, PACK * N], BF16)
-        nc.vector.tensor_copy(
-            out=w3_bf[:].rearrange("p (c i j) -> p c j i", j=PACK, i=4),
-            in_=raw[2][:].rearrange("p j (c i) -> p c j i", i=4),
-        )
-        w3q = quantize("w3", w3_bf[:], N)
+        def hidden(i):
+            start, width = PIECES[i]
+            accs = multiply(f"z{i}", wq[2], width, (0, 2, 3)[i])
+            for t in range(PACK):
+                nc.scalar.activation(out=plain[t][:, start : start + width], in_=accs[t], func=ACT.Tanh)
 
-        def finish(i, banks, per_bank):
+        def gain_h(t, cols):
+            gained(hid[t][:, cols], plain[t][:, cols], t)
+
+        def fetch_h(engine, i, t):
             start, width = OUT_PIECES[i]
-            result = tile(f"result{i}", [P, PACK, width], F32)
-            for b, acc in enumerate(banks):
-                rows = slice(b * per_bank, (b + 1) * per_bank)
-                nc.vector.tensor_tensor(
-                    out=result[:, rows, :].rearrange("p t c -> p (t c)"),
-                    in0=acc[:],
-                    in1=res_sb[i][:, rows, :].rearrange("p t c -> p (t c)"),
-                    op=ALU.add,
-                )
-                nc.sync.dma_start(out_rows[:, rows, start : start + width], result[:, rows, :])
+            fetch(engine, moved[i][:, t, :], hid[t], mv_sb, start, width)
 
-        pending = None
-        for i, (start, width) in enumerate(OUT_PIECES):
-            moved = tile(f"moved{i}", [P, PACK, width], F32)
-            for t in range(PACK):
-                fetch(nc.vector if i == 0 and t < 2 else nc.scalar, moved[:, t, :], hid[t], mv_sb, start, width)
-            z2_bf = gained(f"z2{i}", moved, width)
-            codes, scales = quantize(f"z2{i}", z2_bf[:], width)
-            banks, per_bank = piece_banks((4, 6, 7)[i], "o_ps", i, width)
-            for t in range(PACK):
-                acc = banks[t // per_bank][:, (t % per_bank) * width : (t % per_bank + 1) * width]
-                product(acc, w3q, t, codes[:], scales[:])
-            if pending is not None:
-                finish(*pending)
-            pending = (i, banks, per_bank)
-        finish(*pending)
+        def project(i):
+            multiply(f"zz{i}", wq[3], OUT_PIECES[i][1], (4, 6, 7)[i])
+
+        def finish(i, b):
+            start, width = OUT_PIECES[i]
+            per_bank = 512 // width
+            result = tile(f"result{i}{b}", [P, per_bank, width], F32)
+            rows = slice(b * per_bank, (b + 1) * per_bank)
+            nc.vector.tensor_tensor(
+                out=result[:].rearrange("p t c -> p (t c)"),
+                in0=sums[f"zz{i}"][b][:],
+                in1=res_sb[i][:, rows, :].rearrange("p t c -> p (t c)"),
+                op=ALU.add,
+            )
+            nc.sync.dma_start(out_rows[:, rows, start : start + width], result[:])
+
+        last = PIECES[-1][0]
+        fetch_y(nc.scalar, 0)
+        fetch_y(nc.scalar, 1)
+        fetch_y(nc.scalar, 2)
+        round_w2(0)
+        add_next(0, 0)
+        fetch_y(nc.vector, 3)
+        add_next(0, 2)
+        add_next(1)
+        add_next(3)
+        add_next(2)
+        fetch_p(nc.scalar, 0)
+        fetch_p(nc.scalar, 1)
+        fetch_p(nc.scalar, 3)
+        fetch_p(nc.scalar, 2)
+        keep_larger(0)
+        round_w2(1)
+        gain_r2(0)
+        keep_larger(1)
+        wq[2] = quantize("w2", w2_bf[:], H)
+        gain_r2(1)
+        keep_larger(3)
+        keep_larger(2)
+        gain_r2(3)
+        gain_r2(2)
+        subtract_next(nc.scalar, 0, 0)
+        subtract_next(nc.scalar, 0, 1)
+        round_w3(0)
+        subtract_next(nc.scalar, 0, 3)
+        round_w3(1)
+        subtract_next(nc.scalar, 0, 2)
+        subtract_next(nc.scalar, 1, 0)
+        weave("z0", diff[0], PIECES[0][1])
+        subtract_next(nc.scalar, 1, 1)
+        hidden(0)
+        subtract_next(nc.scalar, 1, 3)
+        subtract_next(nc.scalar, 1, 2)
+        subtract_next(nc.scalar, 2, 0)
+        weave("z1", diff[1], PIECES[1][1])
+        subtract_next(nc.scalar, 2, 1)
+        hidden(1)
+        subtract_next(nc.scalar, 2, 3)
+        subtract_next(nc.scalar, 2, 2)
+        round_w3(2)
+        weave("z2", diff[2], PIECES[2][1])
+        round_w3(3)
+        hidden(2)
+        gain_h(0, slice(0, last))
+        gain_h(1, slice(0, last))
+        gain_h(2, slice(0, last))
+        gain_h(3, slice(0, last))
+        gain_h(0, slice(last, S))
+        gain_h(1, slice(last, S))
+        gain_h(2, slice(last, S))
+        gain_h(3, slice(last, S))
+        fetch_h(nc.scalar, 0, 0)
+        fetch_h(nc.scalar, 0, 1)
+        fetch_h(nc.vector, 0, 2)
+        fetch_h(nc.vector, 0, 3)
+        fetch_h(nc.vector, 1, 3)
+        wq[3] = quantize("w3", w3_bf[:], N)
+        fetch_h(nc.scalar, 1, 0)
+        fetch_h(nc.scalar, 1, 1)
+        fetch_h(nc.scalar, 1, 2)
+        fetch_h(nc.scalar, 2, 0)
+        fetch_h(nc.scalar, 2, 1)
+        fetch_h(nc.scalar, 2, 2)
+        fetch_h(nc.scalar, 2, 3)
+        weave("zz0", moved[0], OUT_PIECES[0][1])
+        weave("zz1", moved[1], OUT_PIECES[1][1])
+        project(0)
+        project(1)
+        weave("zz2", moved[2], OUT_PIECES[2][1])
+        finish(0, 0)
+        project(2)
+        finish(0, 1)
+        finish(1, 0)
+        finish(2, 0)

from contextlib import ExitStack

import concourse.mybir as mybir

K, T, S, H, N = 512, 2048, 512, 512, 512
FLOPS = 2 * K * H * S + 2 * H * H * S + 2 * H * N * S

F32 = mybir.dt.float32
BF16 = mybir.dt.bfloat16
I32 = mybir.dt.int32
U32 = mybir.dt.uint32
U16 = mybir.dt.uint16
U8 = mybir.dt.uint8
FP8X4 = mybir.dt.float8_e4m3fn_x4
ALU = mybir.AluOpType
ACT = mybir.ActivationFunctionType

P = 128
PACK = 4
HALF = S // 2
PIECES = ((0, 256), (256, 128), (384, 128))
OUT_PIECES = ((0, 256), (256, 128), (384, 128))
W1_SCALAR_SHARE = 64


def tile_picked_alldbl3_none_p_kernel(
    tc, x_words, x_scales, w1, gn, w2, res, w3, offs, nx, mv, out
):
    nc = tc.nc
    with ExitStack() as ctx:
        sb = ctx.enter_context(tc.tile_pool(name="sb", bufs=1))
        ps = ctx.enter_context(tc.psum_pool(name="ps", bufs=1))

        def tile(name, shape, dtype):
            return sb.tile(shape, dtype, name=name, align_bytes=64)

        def bank(number, name):
            return ps.tile([P, 512], F32, name=name, tag=f"bank{number}")

        def entries(lists, start, count):
            return lists[:, start // 16 : (start + count) // 16]

        def fetch(engine, dst, window, lists, start, count):
            src = window[:].indirect(entries(lists, start, count))
            if engine is nc.vector:
                nc.vector.tensor_copy(out=dst, in_=src)
            else:
                nc.scalar.activation(out=dst, in_=src, func=ACT.Copy)

        def quantize(name, values, width):
            codes = tile(name + "_codes", [P, width], U32)
            scales = tile(name + "_scales", [P, width], U8)
            nc.vector.quantize_mx(out=codes[:].bitcast(FP8X4), scales=scales[:], in_=values)
            return codes, scales

        def product(dst, weights, t, codes, scales):
            cols = slice(P * t, P * (t + 1))
            nc.tensor.matmul_mx(
                out=dst,
                lhsT=weights[0][:, cols].bitcast(FP8X4),
                lhsT_scale=weights[1][:, cols],
                rhs=codes.bitcast(FP8X4),
                rhs_scale=scales,
                start=True,
                stop=True,
            )

        offs_sb = sb.tile([P, S // 16], U16, name="offs_sb")
        nx_sb = sb.tile([P, S // 16], U16, name="nx_sb")
        mv_sb = sb.tile([P, S // 16], U16, name="mv_sb")
        x_sb = tile("x_sb", [P, T], I32)
        xs_sb = tile("xs_sb", [P, T], U8)
        gain = tile("gain", [P, PACK], F32)
        raw = [tile(f"raw{i}", [P, PACK, 512], F32) for i in range(3)]
        res_sb = [tile(f"res{i}", [P, PACK, width], F32) for i, (start, width) in enumerate(OUT_PIECES)]

        nc.vector.memset(xs_sb[:].bitcast(I32), 0)
        nc.sync.dma_start(offs_sb[:], offs)
        nc.sync.dma_start(raw[0][:], w1.rearrange("(p j) c -> p j c", j=PACK))
        for q in range(4):
            nc.sync.dma_start(
                xs_sb[32 * q : 32 * q + 4, :].bitcast(I32), x_scales[0, 4 * q : 4 * q + 4, :].bitcast(I32)
            )
        nc.sync.dma_start(x_sb[:], x_words[0].rearrange("p c r -> p (c r)").bitcast(I32))
        nc.sync.dma_start(nx_sb[:], nx)
        nc.sync.dma_start(raw[1][:], w2.rearrange("(p j) c -> p j c", j=PACK))
        nc.sync.dma_start(gain[:], gn.rearrange("(p t) o -> p (t o)", t=PACK))
        nc.sync.dma_start(raw[2][:], w3.rearrange("(p j) c -> p j c", j=PACK))
        nc.sync.dma_start(mv_sb[:], mv)
        res_rows = res.rearrange("(t p) c -> p t c", p=P)
        out_rows = out.rearrange("(t p) c -> p t c", p=P)
        for i, (start, width) in enumerate(OUT_PIECES):
            nc.sync.dma_start(res_sb[i][:], res_rows[:, :, start : start + width])

        def dealt_views(i, rounded):
            dst = rounded[:].rearrange("p (t m j) -> p m j t", t=PACK, j=PACK)
            src = raw[i][:].rearrange("p j (m t) -> p m j t", t=PACK)
            return dst, src

        xq_scales = tile("xq_scales", [P, S], U8)
        nc.vector.tensor_copy(out=xq_scales[:], in_=xs_sb[:].indirect(offs_sb[:]))

        w1_bf = tile("w1_bf", [P, PACK * H], BF16)
        dst, src = dealt_views(0, w1_bf)
        nc.scalar.copy(out=dst[:, :W1_SCALAR_SHARE], in_=src[:, :W1_SCALAR_SHARE])
        nc.vector.tensor_copy(out=dst[:, W1_SCALAR_SHARE:], in_=src[:, W1_SCALAR_SHARE:])
        w1q = quantize("w1", w1_bf[:], H)

        xq = tile("xq", [P, S], U32)
        halves = [slice(h * HALF, (h + 1) * HALF) for h in range(2)]
        for h in range(2):
            nc.vector.tensor_copy(out=xq[:, halves[h]], in_=x_sb[:].bitcast(U32).indirect(entries(offs_sb, h * HALF, HALF)))

        y = [tile(f"y{t}", [P, S], F32) for t in range(PACK)]
        y_parts = [(0, halves[0]), (1, halves[0]), (0, halves[1]), (1, halves[1]), (2, slice(0, S)), (3, slice(0, S))]
        y_ps = []
        for b, (t, cols) in enumerate(y_parts):
            y_ps.append(bank(b, f"y_ps{b}")[:, cols])
            product(y_ps[b], w1q, t, xq[:, cols], xq_scales[:, cols])
            if b in (0, 1):
                nc.scalar.copy(out=y[t][:, cols], in_=y_ps[b])
            else:
                nc.vector.tensor_copy(out=y[t][:, cols], in_=y_ps[b])

        y_next = [tile(f"y_next{t}", [P, S], F32) for t in range(PACK)]

        p = [tile(f"p{t}", [P, S], F32) for t in range(PACK)]
        p_next = [tile(f"p_next{t}", [P, S], F32) for t in range(PACK)]
        def gained(dst, src, t):
            nc.vector.tensor_scalar(out=dst, in0=src, scalar1=gain[:, t : t + 1], scalar2=None, op0=ALU.mult)

        def woven(name, planes, width):
            rounded = tile(name, [P, PACK * width], BF16)
            nc.vector.tensor_copy(
                out=rounded[:].rearrange("p (c i t) -> p c t i", t=PACK, i=4),
                in_=planes[:].rearrange("p t (c i) -> p c t i", i=4),
            )
            return rounded

        w2_bf = tile("w2_bf", [P, PACK * H], BF16)
        w3_bf = tile("w3_bf", [P, PACK * N], BF16)
        r2 = [tile(f"r2{t}", [P, S], F32) for t in range(PACK)]
        larger = [tile(f"larger{t}", [P, S], F32) for t in range(PACK)]

        def round_w2(part):
            dst, src = dealt_views(1, w2_bf)
            cols = slice(64 * part, 64 * (part + 1))
            nc.vector.tensor_copy(out=dst[:, cols], in_=src[:, cols])

        def round_w3(part):
            dst = w3_bf[:].rearrange("p (c i j) -> p c j i", j=PACK, i=4)
            src = raw[2][:].rearrange("p j (c i) -> p c j i", i=4)
            cols = slice(32 * part, 32 * (part + 1))
            nc.vector.tensor_copy(out=dst[:, cols], in_=src[:, cols])

        def fetch_y(engine, t):
            for h in range(2):
                fetch(engine, y_next[t][:, halves[h]], y[t], nx_sb, h * HALF, HALF)

        def add_next(t, only=None):
            for b, (part_t, cols) in enumerate(y_parts):
                if part_t == t and only in (None, b):
                    nc.vector.tensor_tensor(out=p[t][:, cols], in0=y_ps[b], in1=y_next[t][:, cols], op=ALU.add)

        def fetch_p(engine, t):
            for h in range(2):
                fetch(engine, p_next[t][:, halves[h]], p[t], nx_sb, h * HALF, HALF)

        def keep_larger(t):
            nc.vector.tensor_tensor(out=larger[t][:], in0=p[t][:], in1=p_next[t][:], op=ALU.max)

        def gain_r2(t):
            gained(r2[t][:], larger[t][:], t)

        hid = [tile(f"h{t}", [P, S], F32) for t in range(PACK)]
        plain = [tile(f"tanh{t}", [P, S], F32) for t in range(PACK)]
        diff = [tile(f"diff{i}", [P, PACK, width], BF16) for i, (start, width) in enumerate(PIECES)]
        moved = [tile(f"moved{i}", [P, PACK, width], BF16) for i, (start, width) in enumerate(OUT_PIECES)]
        rounded = {}
        sums = {}
        wq = {}

        def subtract_next(engine, i, t):
            start, width = PIECES[i]
            r2_next = tile(f"r2_next{t}", [P, width], F32)
            fetch(engine, r2_next[:], r2[t], nx_sb, start, width)
            nc.vector.tensor_tensor(out=diff[i][:, t, :], in0=r2[t][:, start : start + width], in1=r2_next[:], op=ALU.subtract)

        def weave(name, planes, width):
            rounded[name] = woven(name + "_bf", planes, width)

        def multiply(name, weights, width, first):
            codes, scales = quantize(name, rounded[name][:], width)
            per_bank = 512 // width
            banks = [bank(first + b, f"{name}_ps{b}") for b in range(PACK // per_bank)]
            sums[name] = banks
            accs = []
            for t in range(PACK):
                accs.append(banks[t // per_bank][:, (t % per_bank) * width : (t % per_bank + 1) * width])
                product(accs[t], weights, t, codes[:], scales[:])
            return accs

        def hidden(i):
            start, width = PIECES[i]
            accs = multiply(f"z{i}", wq[2], width, (0, 2, 3)[i])
            for t in range(PACK):
                nc.scalar.activation(out=plain[t][:, start : start + width], in_=accs[t], func=ACT.Tanh)

        def gain_h(t, cols):
            gained(hid[t][:, cols], plain[t][:, cols], t)

        def fetch_h(engine, i, t):
            start, width = OUT_PIECES[i]
            fetch(engine, moved[i][:, t, :], hid[t], mv_sb, start, width)

        def project(i):
            multiply(f"zz{i}", wq[3], OUT_PIECES[i][1], (4, 6, 7)[i])

        def finish(i, b):
            start, width = OUT_PIECES[i]
            per_bank = 512 // width
            result = tile(f"result{i}{b}", [P, per_bank, width], F32)
            rows = slice(b * per_bank, (b + 1) * per_bank)
            nc.vector.tensor_tensor(
                out=result[:].rearrange("p t c -> p (t c)"),
                in0=sums[f"zz{i}"][b][:],
                in1=res_sb[i][:, rows, :].rearrange("p t c -> p (t c)"),
                op=ALU.add,
            )
            nc.sync.dma_start(out_rows[:, rows, start : start + width], result[:])

        last = PIECES[-1][0]
        fetch_y(nc.scalar, 0)
        fetch_y(nc.scalar, 1)
        fetch_y(nc.scalar, 2)
        round_w2(0)
        add_next(0, 0)
        fetch_y(nc.vector, 3)
        add_next(0, 2)
        add_next(1)
        add_next(3)
        add_next(2)
        fetch_p(nc.scalar, 0)
        fetch_p(nc.scalar, 1)
        fetch_p(nc.scalar, 3)
        fetch_p(nc.scalar, 2)
        keep_larger(0)
        round_w2(1)
        gain_r2(0)
        keep_larger(1)
        wq[2] = quantize("w2", w2_bf[:], H)
        gain_r2(1)
        keep_larger(3)
        keep_larger(2)
        gain_r2(3)
        gain_r2(2)
        subtract_next(nc.scalar, 0, 0)
        subtract_next(nc.scalar, 0, 1)
        round_w3(0)
        subtract_next(nc.scalar, 0, 3)
        round_w3(1)
        subtract_next(nc.scalar, 0, 2)
        subtract_next(nc.scalar, 1, 0)
        weave("z0", diff[0], PIECES[0][1])
        subtract_next(nc.scalar, 1, 1)
        hidden(0)
        subtract_next(nc.scalar, 1, 3)
        subtract_next(nc.scalar, 1, 2)
        subtract_next(nc.scalar, 2, 0)
        weave("z1", diff[1], PIECES[1][1])
        subtract_next(nc.scalar, 2, 1)
        hidden(1)
        subtract_next(nc.scalar, 2, 3)
        subtract_next(nc.scalar, 2, 2)
        round_w3(2)
        weave("z2", diff[2], PIECES[2][1])
        round_w3(3)
        hidden(2)
        gain_h(0, slice(0, last))
        gain_h(1, slice(0, last))
        gain_h(2, slice(0, last))
        gain_h(3, slice(0, last))
        gain_h(0, slice(last, S))
        gain_h(1, slice(last, S))
        gain_h(2, slice(last, S))
        gain_h(3, slice(last, S))
        fetch_h(nc.scalar, 0, 0)
        fetch_h(nc.scalar, 0, 1)
        fetch_h(nc.vector, 0, 2)
        fetch_h(nc.vector, 0, 3)
        fetch_h(nc.vector, 1, 3)
        wq[3] = quantize("w3", w3_bf[:], N)
        fetch_h(nc.scalar, 1, 0)
        fetch_h(nc.scalar, 1, 1)
        fetch_h(nc.scalar, 1, 2)
        fetch_h(nc.scalar, 2, 0)
        fetch_h(nc.scalar, 2, 1)
        fetch_h(nc.scalar, 2, 2)
        fetch_h(nc.scalar, 2, 3)
        weave("zz0", moved[0], OUT_PIECES[0][1])
        weave("zz1", moved[1], OUT_PIECES[1][1])
        project(0)
        project(1)
        weave("zz2", moved[2], OUT_PIECES[2][1])
        finish(0, 0)
        project(2)
        finish(0, 1)
        finish(1, 0)
        finish(2, 0)
